import numpy as np
import ml_dtypes


def mxq(x, axis, fmt="e4m3"):
    dtype, down = {"e4m3": (ml_dtypes.float8_e4m3fn, 7), "e5m2": (ml_dtypes.float8_e5m2, 14)}[fmt]
    v = np.moveaxis(np.asarray(x, np.float32).astype(ml_dtypes.bfloat16).astype(np.float64), axis, -1)
    blocks = v.reshape(v.shape[:-1] + (-1, 32))
    amax = np.abs(blocks).max(-1, keepdims=True)
    byte = np.maximum(np.where(amax > 0, np.frexp(amax)[1] - 1 + 127, 0) - down, 1)
    scale = np.exp2(byte - 127.0)
    codes = (blocks / scale).astype(np.float32).astype(dtype).astype(np.float64)
    return np.moveaxis((codes * scale).reshape(v.shape), -1, axis)


WIDE = False


def mx_kscale(k):
    if not WIDE:
        return np.ones(k)
    levels = np.array([10, -10, 5, -5, 0])
    if k % 512:
        return np.exp2(np.random.permutation(np.resize(levels, k // 32))).repeat(32)
    a = np.empty((k // 512, 16))
    for p in range(k // 512):
        a[p, :8] = np.random.permutation(np.resize(levels, 8))
        for g in range(8):
            far = levels[np.abs(levels - a[p, g]) >= 10]
            a[p, g + 8] = far[np.random.randint(len(far))]
    return np.exp2(a.ravel()).repeat(32)


def f64(x):
    return np.asarray(x).astype(np.float64)


def striped(idx):
    return np.tile(idx.reshape(-1, 16).T, (8, 1)).astype(np.uint16)


def unstriped(offs):
    return offs[:16].T.reshape(-1).astype(np.int64)


E2M1 = np.array([0.0, 0.5, 1.0, 1.5, 2.0, 3.0, 4.0, 6.0, -0.0, -0.5, -1.0, -1.5, -2.0, -3.0, -4.0, -6.0])


def pack_weight(w, fmt):
    k, n = w.shape
    w = f64(np.asarray(w, np.float32).astype(ml_dtypes.bfloat16)).reshape(k // 32, 32, n)
    amax = np.abs(w).max(1)
    if fmt == "e4m3":
        byte = np.frexp(amax)[1] - 1 + 127 - 7
    else:
        mant, ex = np.frexp(amax / 6.0)
        byte = np.where(mant > 0.5, ex, ex - 1) + 127
    byte = np.clip(np.where(amax > 0, byte, 1), 1, 254)
    scaled = (w * np.exp2(127.0 - byte)[:, None, :]).reshape(k, n).astype(np.float32)
    by_word = np.ascontiguousarray(scaled.reshape(k // 512, 128, 4, n).transpose(0, 1, 3, 2))
    if fmt == "e4m3":
        words = by_word.astype(ml_dtypes.float8_e4m3fn).view(np.uint8)
    else:
        c = by_word.astype(ml_dtypes.float4_e2m1fn).view(np.uint8) & 0xF
        words = (c[..., 0::2] | (c[..., 1::2] << 4)).reshape(k // 512, 128, 2 * n)
    return np.ascontiguousarray(words), np.ascontiguousarray(byte.astype(np.uint8).reshape(k // 512, 16, n))


def unpack_weight(words, scales, fmt):
    g, _, n = scales.shape
    words = np.ascontiguousarray(words).reshape(g, 128, n, -1)
    if fmt == "e4m3":
        vals = words.view(ml_dtypes.float8_e4m3fn).astype(np.float64)
    else:
        nib = np.empty((g, 128, n, 4), np.uint8)
        nib[..., 0::2] = words & 0xF
        nib[..., 1::2] = words >> 4
        vals = E2M1[nib]
    vals = vals * np.repeat(np.exp2(scales.astype(np.float64) - 127.0), 8, axis=1)[..., None]
    return vals.transpose(0, 1, 3, 2).reshape(g * 512, n)


def gelu(v):
    return 0.5 * v * (1.0 + np.tanh(np.sqrt(2.0 / np.pi) * (v + 0.044715 * v**3)))


def twice(P):
    return np.random.permutation(np.repeat(np.arange(P), 2))


K, H, T, S, P = 1536, 1024, 4096, 1024, 512


def setup_inputs():
    n = np.random.standard_normal
    s = mx_kscale(K)[:, None]
    u = mx_kscale(H)[:, None]
    d = {}
    d["tab_words"], d["tab_scales"] = pack_weight(n((K, T)) * s, "e4m3")
    d["offs"] = striped(np.random.permutation(T)[:S])
    perm = np.random.permutation(S)
    d["pos1"] = striped(perm[:P])
    d["pos2"] = striped(perm[P:2 * P])
    d["pos3"] = striped(twice(P))
    d["w1"] = (n((K, H)) / K**0.5 / s * u.T).astype(np.float32)
    d["w2_words"], d["w2_scales"] = pack_weight(n((H, H)) / H**0.5 / u, "e2m1")
    d["low"] = (0.6 * n(H)).astype(np.float32)
    d["own"] = (np.exp(0.3 * n(H)) / u[:, 0]).astype(np.float32)
    d["base"] = (0.6 * n((H, S))).astype(np.float32)
    return d


def reference(tab_words, tab_scales, offs, pos1, pos2, pos3, w1, w2_words, w2_scales, low, own, base):
    v = unpack_weight(tab_words, tab_scales, "e4m3")[:, unstriped(offs)]
    h = mxq(f64(w1), 0, "e4m3").T @ v
    left = h[:, unstriped(pos1)]
    right = h[:, unstriped(pos2)]
    z = np.maximum(left, right) + f64(low)[:, None] * np.minimum(left, right)
    w2 = unpack_weight(w2_words, w2_scales, "e2m1")
    y = w2.T @ mxq(z, 0, "e4m3")
    up = y[:, unstriped(pos3)]
    out = np.minimum(up, f64(own)[:, None] * h) + f64(base)
    return out

from contextlib import ExitStack

import concourse.mybir as mybir

K, H, T, S, M = 1536, 1024, 4096, 1024, 512
FLOPS = 2 * K * H * S + 2 * H * H * M

F32 = mybir.dt.float32
BF16 = mybir.dt.bfloat16
I32 = mybir.dt.int32
U32 = mybir.dt.uint32
U16 = mybir.dt.uint16
U8 = mybir.dt.uint8
FP8X4 = mybir.dt.float8_e4m3fn_x4
FP4X4 = mybir.dt.float4_e2m1fn_x4
ALU = mybir.AluOpType

P = 128
PACK = 4
KP = P * PACK
PASS1 = K // KP
PASS2 = H // KP
TILES = H // P
BANK = 512
Y_PAD = 16
Y_TILES = 4
V_SHARE = 80


def tile_list_udder_half_features_kernel(
    tc, tab_words, tab_scales, offs, pos1, pos2, pos3, w1, w2_words, w2_scales, low, own, base, out
):
    nc = tc.nc
    with ExitStack() as ctx:
        keep = ctx.enter_context(tc.tile_pool(name="keep", bufs=1))
        ring = ctx.enter_context(tc.tile_pool(name="ring", bufs=2))
        psum = ctx.enter_context(tc.psum_pool(name="psum", bufs=1))

        offs_t = keep.tile([P, S // 16], U16, name="offs_t")
        pos1_t = keep.tile([P, M // 16], U16, name="pos1_t")
        pos2_t = keep.tile([P, M // 16], U16, name="pos2_t")
        pos3_t = keep.tile([P, S // 16], U16, name="pos3_t")
        low_t = keep.tile([P, PASS2, PACK], F32, name="low_t")
        own_t = keep.tile([P, PASS2, PACK], F32, name="own_t")
        rest_t = keep.tile([P, PASS2, PACK], F32, name="rest_t")
        tab_t = [keep.tile([P, T], U32, name=f"tab{a}") for a in range(PASS1)]
        tabs_t = keep.tile([P, T], U8, name="tabs_t")
        v_codes = [keep.tile([P, S], U32, name=f"v_codes{a}", align_bytes=64) for a in range(PASS1)]
        v_scales = keep.tile([P, S], U8, name="v_scales", align_bytes=64)
        w2w_raw = keep.tile([P, PASS2, 2 * H], U8, name="w2w_raw")
        w2s_raw = keep.tile([P, PASS2, H], U8, name="w2s_raw")
        base_t = [keep.tile([P, PACK, S], F32, name=f"base{b}") for b in range(PASS2)]
        h_t = [keep.tile([P, S], F32, name=f"h{i}") for i in range(TILES)]
        y_t = [keep.tile([P, M + Y_PAD], F32, name=f"y{i}") for i in range(Y_TILES)]
        up_t = [keep.tile([P, BANK], F32, name=f"up{i}") for i in range(2)]

        nc.vector.memset(tabs_t[:].bitcast(I32), 0)
        nc.vector.memset(w2s_raw[:].rearrange("p a c -> p (a c)").bitcast(I32), 0)
        for i in range(Y_TILES):
            nc.vector.memset(y_t[i][:, M:], 0.0)

        nc.sync.dma_start(offs_t[:], offs)
        tab_i32 = [tab_words[a].rearrange("p t i -> p (t i)").bitcast(I32) for a in range(PASS1)]
        nc.sync.dma_start(tab_t[0][:].bitcast(I32), tab_i32[0])
        tabs_i32 = tab_scales.bitcast(I32)
        for q in range(4):
            nc.sync.dma_start(tabs_t[32 * q : 32 * q + 4 * PASS1, :].bitcast(I32), tabs_i32[:, 4 * q : 4 * q + 4, :])
        for a in range(1, PASS1):
            nc.sync.dma_start(tab_t[a][:].bitcast(I32), tab_i32[a])

        w2s_i32 = w2_scales.bitcast(I32)
        for q in range(4):
            nc.sync.dma_start(
                w2s_raw[32 * q : 32 * q + 4].bitcast(I32),
                w2s_i32[:, 4 * q : 4 * q + 4, :].rearrange("a r c -> r a c"),
            )
        w2s = keep.tile([P, 2 * PASS2, PACK, P], U8, name="w2s", align_bytes=64)
        nc.gpsimd.tensor_copy(
            w2s[:], w2s_raw[:].rearrange("p a (b m t) -> p (a b) t m", b=PASS2, t=PACK)
        )

        def load_w1(a, b):
            raw = ring.tile([P, PACK, KP], F32, name="raw", tag="raw", bufs=3)
            rows = w1[KP * a : KP * (a + 1), KP * b : KP * (b + 1)]
            nc.sync.dma_start(raw[:], rows.rearrange("(p j) c -> p j c", j=PACK))
            return raw

        def cast_w1(raw, shares):
            grouped = ring.tile([P, PACK, P, PACK], BF16, name="grouped", tag="grouped", align_bytes=64)
            src = raw[:].rearrange("p j (m t) -> p m j t", t=PACK)
            dst = grouped[:].rearrange("p t m j -> p m j t")
            for copy, m0, m1 in shares:
                copy(dst[:, m0:m1], src[:, m0:m1])
            return grouped

        def quantize(grouped_flat, name, cuts):
            codes = keep.tile([P, KP], U32, name=f"{name}_codes", align_bytes=64)
            scales = keep.tile([P, KP], U8, name=f"{name}_scales", align_bytes=64)
            for c0, c1 in cuts:
                nc.vector.quantize_mx(
                    out=codes[:, c0:c1].bitcast(FP8X4),
                    scales=scales[:, c0:c1],
                    in_=grouped_flat[:, PACK * c0 : PACK * c1],
                )
            return codes, scales

        raws = {(a, 0): load_w1(a, 0) for a in range(PASS1)}
        nc.sync.dma_start(pos1_t[:], pos1)
        nc.sync.dma_start(pos2_t[:], pos2)
        nc.sync.dma_start(low_t[:], low.rearrange("(b p t) -> p b t", b=PASS2, t=PACK))

        nc.vector.tensor_copy(v_codes[0][:], tab_t[0][:].indirect(offs_t[:]))
        nc.vector.tensor_copy(v_scales[:], tabs_t[:].indirect(offs_t[:]))
        for a in range(1, PASS1):
            nc.vector.tensor_copy(v_codes[a][:], tab_t[a][:].indirect(offs_t[:]))
        nc.vector.tensor_scalar(rest_t[:], low_t[:], -1.0, None, ALU.add)

        whole = [(0, KP)]
        first_out = [(0, P), (P, 2 * P), (2 * P, KP)]
        shared = [(nc.vector.tensor_copy, 0, V_SHARE), (nc.scalar.copy, V_SHARE, P)]
        scalar_only = [(nc.scalar.copy, 0, P)]

        def stage1(b, shares):
            banks = [psum.tile([P, BANK], F32, name=f"bank{n}", tag=f"bank{n}") for n in range(8)]
            for a in range(PASS1):
                grouped = cast_w1(raws[a, b], shares)
                cuts = first_out if a == PASS1 - 1 else whole
                codes, scales = quantize(grouped[:].rearrange("p t m j -> p (t m j)"), f"w1_{a}_{b}", cuts)
                for t in range(PACK):
                    for half in range(2):
                        cols = slice(BANK * half, BANK * (half + 1))
                        nc.tensor.matmul_mx(
                            out=banks[2 * t + half][:],
                            lhsT=codes[:, P * t : P * (t + 1)].bitcast(FP8X4),
                            lhsT_scale=scales[:, P * t : P * (t + 1)],
                            rhs=v_codes[a][:, cols].bitcast(FP8X4),
                            rhs_scale=v_scales[4 * a :, cols],
                            start=(a == 0),
                            stop=(a == PASS1 - 1),
                        )
            for t in range(PACK):
                for half in range(2):
                    copy = nc.vector.tensor_copy if (b, t, half) == (0, 0, 1) else nc.scalar.copy
                    copy(h_t[PACK * b + t][:, BANK * half : BANK * (half + 1)], banks[2 * t + half][:])

        stage1(0, shared)

        for a in range(PASS1):
            raws[a, 1] = load_w1(a, 1)
        nc.sync.dma_start(
            w2w_raw[:].bitcast(I32), w2_words.bitcast(I32).rearrange("a p c -> p a c")
        )
        nc.sync.dma_start(pos3_t[:], pos3)
        nc.sync.dma_start(own_t[:], own.rearrange("(b p t) -> p b t", b=PASS2, t=PACK))
        base_rows = base.rearrange("(b p t) j -> b p t j", b=PASS2, t=PACK)
        out_rows = out.rearrange("(b p t) j -> b p t j", b=PASS2, t=PACK)
        for b in range(PASS2):
            nc.sync.dma_start(base_t[b][:], base_rows[b])

        stage1(1, scalar_only)

        planes = [ring.tile([P, PACK, M], BF16, name="planes", tag="planes") for b in range(PASS2)]
        picked = {-1: ring.tile([P, 2, M], F32, name="lr", tag="lr", align_bytes=64, bufs=3)}
        zq = {}

        def finish_z(i):
            b, t = divmod(i, PACK)
            nc.vector.scalar_tensor_tensor(
                planes[b][:, t, :], picked[i - 1][:, 0, :], rest_t[:, b, t : t + 1], picked[i][:, 1, :], ALU.mult, ALU.add
            )

        def weave_z(b, shares):
            grouped = ring.tile([P, M, PACK], BF16, name="grouped", tag="grouped", align_bytes=64)
            src = planes[b][:].rearrange("p t (c i) -> p c t i", i=4)
            dst = grouped[:].rearrange("p (c i) t -> p c t i", i=4)
            for copy, c0, c1 in shares:
                copy(dst[:, c0:c1], src[:, c0:c1])
            return grouped

        for i in range(TILES):
            b, t = divmod(i, PACK)
            lr = ring.tile([P, 2, M], F32, name="lr", tag="lr", align_bytes=64, bufs=3)
            picked[i] = lr
            nc.vector.tensor_copy(lr[:, 0, :], h_t[i][:].indirect(pos1_t[:]))
            nc.vector.tensor_copy(lr[:, 1, :], h_t[i][:].indirect(pos2_t[:]))
            if i > 0:
                finish_z(i - 1)
            nc.vector.tensor_tensor(picked[i - 1][:, 0, :], lr[:, 0, :], lr[:, 1, :], ALU.min)
            nc.gpsimd.tensor_tensor(lr[:, 1, :], lr[:, 0, :], lr[:, 1, :], ALU.add)
            if i == PACK:
                grouped = weave_z(0, scalar_only)
                zq[0] = quantize(grouped[:].rearrange("p m t -> p (m t)"), "z0", whole)

        w2w = ring.tile([P, 2 * PASS2, PACK, P], U16, name="w2w", tag="lr", align_bytes=64, bufs=3)
        nc.vector.tensor_copy(
            w2w[:].rearrange("p g t m -> p g m t"),
            w2w_raw[:].bitcast(U16).rearrange("p a (b m t) -> p (a b) m t", b=PASS2, t=PACK),
        )
        finish_z(TILES - 1)
        grouped = weave_z(1, [(nc.vector.tensor_copy, 64, 128), (nc.vector.tensor_copy, 40, 64), (nc.scalar.copy, 0, 40)])
        zq[1] = quantize(grouped[:].rearrange("p m t -> p (m t)"), "z1", [(256, 512), (0, 256)])

        banks = [psum.tile([P, BANK], F32, name=f"bank{n}", tag=f"bank{n}") for n in range(TILES)]
        for a in range(PASS2):
            codes, scales = zq[a]
            for i in range(TILES):
                b, t = divmod(i, PACK)
                nc.tensor.matmul_mx(
                    out=banks[i][:],
                    lhsT=w2w[:, PASS2 * a + b, t, :].bitcast(FP4X4),
                    lhsT_scale=w2s[:, PASS2 * a + b, t, :],
                    rhs=codes[:].bitcast(FP8X4),
                    rhs_scale=scales[:],
                    start=(a == 0),
                    stop=(a == PASS2 - 1),
                )
        for i in range(TILES):
            b, t = divmod(i, PACK)
            y = y_t[i % Y_TILES]
            nc.scalar.copy(y[:, :M], banks[i][:])
            least = ring.tile([P, S], F32, name="least", tag="raw", bufs=3)
            for half in range(2):
                nc.vector.tensor_copy(up_t[half][:], y[:].indirect(pos3_t[:, 32 * half : 32 * (half + 1)]))
            for half in range(2):
                cols = slice(BANK * half, BANK * (half + 1))
                nc.vector.scalar_tensor_tensor(
                    least[:, cols], h_t[i][:, cols], own_t[:, b, t : t + 1], up_t[half][:], ALU.mult, ALU.min
                )
            if i < TILES - 1:
                nc.gpsimd.tensor_tensor(base_t[b][:, t, :], least[:], base_t[b][:, t, :], ALU.add)
                nc.sync.dma_start(out_rows[b][:, t, :], base_t[b][:, t, :])
            else:
                for half in range(2):
                    cols = slice(BANK * half, BANK * (half + 1))
                    nc.vector.tensor_tensor(base_t[b][:, t, cols], least[:, cols], base_t[b][:, t, cols], ALU.add)
                    nc.sync.dma_start(out_rows[b][:, t, cols], base_t[b][:, t, cols])
